import numpy as np
import ml_dtypes


def mxq(x, axis, fmt="e4m3"):
    dtype, down = {"e4m3": (ml_dtypes.float8_e4m3fn, 7), "e5m2": (ml_dtypes.float8_e5m2, 14)}[fmt]
    v = np.moveaxis(np.asarray(x, np.float32).astype(ml_dtypes.bfloat16).astype(np.float64), axis, -1)
    blocks = v.reshape(v.shape[:-1] + (-1, 32))
    amax = np.abs(blocks).max(-1, keepdims=True)
    byte = np.maximum(np.where(amax > 0, np.frexp(amax)[1] - 1 + 127, 0) - down, 1)
    scale = np.exp2(byte - 127.0)
    codes = (blocks / scale).astype(np.float32).astype(dtype).astype(np.float64)
    return np.moveaxis((codes * scale).reshape(v.shape), -1, axis)


WIDE = False


def mx_kscale(k):
    if not WIDE:
        return np.ones(k)
    levels = np.array([10, -10, 5, -5, 0])
    if k % 512:
        return np.exp2(np.random.permutation(np.resize(levels, k // 32))).repeat(32)
    a = np.empty((k // 512, 16))
    for p in range(k // 512):
        a[p, :8] = np.random.permutation(np.resize(levels, 8))
        for g in range(8):
            far = levels[np.abs(levels - a[p, g]) >= 10]
            a[p, g + 8] = far[np.random.randint(len(far))]
    return np.exp2(a.ravel()).repeat(32)


def f64(x):
    return np.asarray(x).astype(np.float64)


def striped(idx):
    return np.tile(idx.reshape(-1, 16).T, (8, 1)).astype(np.uint16)


def unstriped(offs):
    return offs[:16].T.reshape(-1).astype(np.int64)


E2M1 = np.array([0.0, 0.5, 1.0, 1.5, 2.0, 3.0, 4.0, 6.0, -0.0, -0.5, -1.0, -1.5, -2.0, -3.0, -4.0, -6.0])


def pack_weight(w, fmt):
    k, n = w.shape
    w = f64(np.asarray(w, np.float32).astype(ml_dtypes.bfloat16)).reshape(k // 32, 32, n)
    amax = np.abs(w).max(1)
    if fmt == "e4m3":
        byte = np.frexp(amax)[1] - 1 + 127 - 7
    else:
        mant, ex = np.frexp(amax / 6.0)
        byte = np.where(mant > 0.5, ex, ex - 1) + 127
    byte = np.clip(np.where(amax > 0, byte, 1), 1, 254)
    scaled = (w * np.exp2(127.0 - byte)[:, None, :]).reshape(k, n).astype(np.float32)
    by_word = np.ascontiguousarray(scaled.reshape(k // 512, 128, 4, n).transpose(0, 1, 3, 2))
    if fmt == "e4m3":
        words = by_word.astype(ml_dtypes.float8_e4m3fn).view(np.uint8)
    else:
        c = by_word.astype(ml_dtypes.float4_e2m1fn).view(np.uint8) & 0xF
        words = (c[..., 0::2] | (c[..., 1::2] << 4)).reshape(k // 512, 128, 2 * n)
    return np.ascontiguousarray(words), np.ascontiguousarray(byte.astype(np.uint8).reshape(k // 512, 16, n))


def unpack_weight(words, scales, fmt):
    g, _, n = scales.shape
    words = np.ascontiguousarray(words).reshape(g, 128, n, -1)
    if fmt == "e4m3":
        vals = words.view(ml_dtypes.float8_e4m3fn).astype(np.float64)
    else:
        nib = np.empty((g, 128, n, 4), np.uint8)
        nib[..., 0::2] = words & 0xF
        nib[..., 1::2] = words >> 4
        vals = E2M1[nib]
    vals = vals * np.repeat(np.exp2(scales.astype(np.float64) - 127.0), 8, axis=1)[..., None]
    return vals.transpose(0, 1, 3, 2).reshape(g * 512, n)


def gelu(v):
    return 0.5 * v * (1.0 + np.tanh(np.sqrt(2.0 / np.pi) * (v + 0.044715 * v**3)))


def striped8(idx):
    return np.concatenate([v.reshape(-1, 16).T for v in idx]).astype(np.uint16)


def unstriped8(offs):
    return np.stack([offs[16 * g:16 * g + 16].T.reshape(-1) for g in range(8)]).astype(np.int64)


def heads(h, wgt, idx8):
    r = np.arange(h.shape[0])
    return wgt[r // 4 % 128] * h[r[:, None], idx8[r % 512 // 64]]


def put_heads(h, wgs, idx8, t2):
    r = np.arange(h.shape[0])
    page = np.zeros((h.shape[0], t2))
    page[r[:, None], idx8[r % 512 // 64]] = wgs[r // 4 % 128] * h
    return page


K, H, N, T, S, P, T2 = 1024, 1024, 512, 4096, 1024, 1024, 2048

def setup_inputs():
    n = np.random.standard_normal
    s = mx_kscale(K)[:, None]
    u = mx_kscale(H)[:, None]
    d = {}
    d["tab_words"], d["tab_scales"] = pack_weight(n((K, T)) * s, "e4m3")
    d["offs"] = striped(np.random.permutation(T)[:S])
    d["offs2"] = striped8(np.stack([np.random.permutation(T2)[:S] for _ in range(8)]))
    d["offs3"] = striped8(np.stack([np.random.permutation(T2)[:P] for _ in range(8)]))
    d["w1"] = (0.8 * n((K, H)) / K ** 0.5 / s).astype(np.float32)
    d["w4_words"], d["w4_scales"] = pack_weight(0.8 * n((K, H)) / K ** 0.5 / s, "e2m1")
    d["vigour"] = (0.7 * np.exp(0.3 * n(H)) * u[:, 0]).astype(np.float32)
    d["wgs"] = np.repeat(np.random.uniform(0.5, 2.0, (8, S)), 16, axis=0).astype(np.float32)
    d["wgt"] = np.repeat(np.random.uniform(0.5, 2.0, (8, P)), 16, axis=0).astype(np.float32)
    d["lim"] = ((0.5 + n((H, P))) * u).astype(np.float32)
    d["w2_words"], d["w2_scales"] = pack_weight(n((H, N)) / H ** 0.5 / u, "e4m3")
    return d

def reference(tab_words, tab_scales, offs, offs2, offs3, w1, w4_words, w4_scales, vigour, wgs, wgt, lim, w2_words, w2_scales):
    v = unpack_weight(tab_words, tab_scales, "e4m3")[:, unstriped(offs)]
    a = mxq(f64(w1), 0, "e4m3").T @ v
    b = unpack_weight(w4_words, w4_scales, "e2m1").T @ v
    h = (a * b + a + b) * f64(vigour)[:, None]
    page = put_heads(h, f64(wgs), unstriped8(offs2), T2)
    x = heads(page, f64(wgt), unstriped8(offs3))
    z = np.minimum(x, f64(lim))
    zq = mxq(z, 0, "e4m3")
    return unpack_weight(w2_words, w2_scales, "e4m3").T @ zq

@@ -1,0 +1,302 @@
+from contextlib import ExitStack
+
+import concourse.mybir as mybir
+from concourse.masks import make_identity
+
+K, H, N, T, S, M, T2 = 1024, 1024, 512, 4096, 1024, 1024, 2048
+FLOPS = 2 * (2 * K * H * S + H * N * M)
+
+F32 = mybir.dt.float32
+BF16 = mybir.dt.bfloat16
+I32 = mybir.dt.int32
+U32 = mybir.dt.uint32
+U16 = mybir.dt.uint16
+U8 = mybir.dt.uint8
+FP8X4 = mybir.dt.float8_e4m3fn_x4
+FP4X4 = mybir.dt.float4_e2m1fn_x4
+ALU = mybir.AluOpType
+COPY = mybir.ActivationFunctionType.Copy
+
+P = 128
+PACK = 4
+PASS = P * PACK
+PASSES = K // PASS
+BANK = 512
+PER_COL = 16
+TAIL = 256
+
+
+def tile_list_oyster_flush_scores_kernel(
+    tc, tab_words, tab_scales, offs, offs2, offs3, w1, w4_words, w4_scales, vigour, wgs, wgt, lim, w2_words, w2_scales, out
+):
+    nc = tc.nc
+    with ExitStack() as ctx:
+        lists = ctx.enter_context(tc.tile_pool(name="lists", bufs=1))
+        keep = ctx.enter_context(tc.tile_pool(name="keep", bufs=1))
+        psum = ctx.enter_context(tc.psum_pool(name="psum", bufs=1))
+
+        def bank(name, number):
+            return psum.tile([P, BANK], F32, name=name, tag="bank%d" % (number % 8))
+
+        def entries(lst, first, count):
+            return lst[:, first // PER_COL : (first + count) // PER_COL]
+
+        pick = lists.tile([P, S // PER_COL], U16, name="pick")
+        put = lists.tile([P, S // PER_COL], U16, name="put")
+        read = lists.tile([P, M // PER_COL], U16, name="read")
+
+        tab_sc = keep.tile([P, T], U8, name="tab_sc", align_bytes=64)
+        w4_sc = keep.tile([P, PASSES, H], U8, name="w4_sc", align_bytes=64)
+        w2_sc = keep.tile([P, N], U8, name="w2_sc", align_bytes=64)
+        v_sc = keep.tile([P, S], U8, name="v_sc", align_bytes=64)
+        v_sc1 = keep.tile([P, S], U8, name="v_sc1", align_bytes=64)
+        ident = keep.tile([P, P], F32, name="ident")
+
+        nc.vector.memset(tab_sc[:].bitcast(I32), 0)
+        nc.vector.memset(w4_sc[:].rearrange("p a n -> p (a n)").bitcast(I32), 0)
+        nc.vector.memset(v_sc1[:].bitcast(I32), 0)
+        nc.vector.memset(w2_sc[:].bitcast(I32), 0)
+        make_identity(nc, ident[:])
+
+        def load_words(a):
+            words = keep.tile([P, T], I32, name="tab_w%d" % a, tag="big", bufs=2)
+            nc.sync.dma_start(words[:], tab_words[a].rearrange("p t i -> p (t i)").bitcast(I32))
+            return words
+
+        def load_w1(b, a):
+            raw = keep.tile([P, PACK, BANK], F32, name="w1_raw%d%d" % (b, a), tag="slot%d%d" % (b, a), align_bytes=64)
+            nc.sync.dma_start(
+                raw[:], w1[a * PASS : (a + 1) * PASS, b * PASS : (b + 1) * PASS].rearrange("(p i) c -> p i c", i=PACK)
+            )
+            return raw
+
+        nc.sync.dma_start(pick[:], offs)
+        tab_w = [load_words(0)]
+        for q in range(4):
+            nc.gpsimd.dma_start(tab_sc[32 * q : 32 * q + 8, :].bitcast(I32), tab_scales[:, 4 * q : 4 * q + 4, :].bitcast(I32))
+        w1_raw = {(0, a): load_w1(0, a) for a in range(PASSES)}
+        for q in range(4):
+            nc.gpsimd.dma_start(
+                w4_sc[32 * q : 32 * q + 4, :, :].bitcast(I32),
+                w4_scales[:, 4 * q : 4 * q + 4, :].rearrange("a r n -> r a n").bitcast(I32),
+            )
+        w4_w = keep.tile([P, PASSES, 2 * H], U8, name="w4_w", align_bytes=64)
+        nc.sync.dma_start(w4_w[:].bitcast(I32), w4_words.rearrange("a p c -> p a c").bitcast(I32))
+        tab_w.append(load_words(1))
+        gain = keep.tile([P, PASSES, PACK], F32, name="gain")
+        nc.sync.dma_start(gain[:], vigour.rearrange("(b p t) -> p b t", p=P, t=PACK))
+        nc.sync.dma_start(put[:], offs2)
+        wgs_sb = keep.tile([P, S], F32, name="wgs_sb")
+        nc.sync.dma_start(wgs_sb[:], wgs)
+        for a in range(PASSES):
+            w1_raw[(1, a)] = load_w1(1, a)
+        nc.sync.dma_start(read[:], offs3)
+        wgt_sb = keep.tile([P, M], F32, name="wgt_sb")
+        nc.sync.dma_start(wgt_sb[:], wgt)
+
+        v_w = [keep.tile([P, S], U32, name="v_w%d" % a, align_bytes=64) for a in range(PASSES)]
+        nc.vector.tensor_copy(v_sc[:], tab_sc[:].indirect(pick[:]))
+        nc.gpsimd.dma_start(v_sc1[0:124, :].bitcast(I32), v_sc[4:128, :].bitcast(I32))
+        nc.vector.tensor_copy(v_w[0][:], tab_w[0][:].bitcast(U32).indirect(pick[:]))
+
+        w1_codes, w1_sc = {}, {}
+
+        def quantise_w1(b, a):
+            grouped = keep.tile([P, BANK, PACK], BF16, name="w1_bf%d%d" % (b, a), tag="w1_bf", bufs=2, align_bytes=64)
+            nc.scalar.copy(grouped[:], w1_raw[(b, a)][:].rearrange("p i c -> p c i"))
+            w1_codes[(b, a)] = keep.tile([P, BANK], U32, name="w1_codes%d%d" % (b, a), align_bytes=64)
+            w1_sc[(b, a)] = keep.tile([P, BANK], U8, name="w1_sc%d%d" % (b, a), align_bytes=64)
+            nc.vector.quantize_mx(
+                out=w1_codes[(b, a)][:].bitcast(FP8X4), scales=w1_sc[(b, a)][:], in_=grouped[:].rearrange("p c i -> p (c i)")
+            )
+
+        pages = []
+        for a in range(PASSES):
+            quantise_w1(0, a)
+            pages.append(keep.tile([P, T2], F32, name="page%d" % a, tag="slot0%d" % a, align_bytes=64))
+            nc.vector.memset(pages[a][:], 0.0)
+        for half in range(2):
+            nc.vector.tensor_copy(
+                v_w[1][:, half * BANK : (half + 1) * BANK], tab_w[1][:].bitcast(U32).indirect(entries(pick, half * BANK, BANK))
+            )
+
+        lim_sb = []
+        for b in range(PASSES):
+            lim_b = keep.tile([P, PACK, M], F32, name="lim%d" % b, tag="big", bufs=2)
+            nc.sync.dma_start(lim_b[:], lim[b * PASS : (b + 1) * PASS, :].rearrange("(p t) m -> p t m", t=PACK))
+            lim_sb.append(lim_b)
+        w2_w = keep.tile([P, PASSES, N], U32, name="w2_w", align_bytes=64)
+        nc.sync.dma_start(w2_w[:].bitcast(I32), w2_words.rearrange("a p c i -> p a (c i)").bitcast(I32))
+        for q in range(4):
+            nc.sync.dma_start(w2_sc[32 * q : 32 * q + 8, :].bitcast(I32), w2_scales[:, 4 * q : 4 * q + 4, :].bitcast(I32))
+
+        h, terms = {}, {}
+
+        def first_stage(b, half):
+            prod = keep.tile([P, 4, BANK], F32, name="prod%d%d" % (b, half), tag="prod", bufs=4)
+            b_sb = keep.tile([P, 4, BANK], F32, name="b_sb%d%d" % (b, half), tag="b_sb", bufs=4)
+            terms[(b, half)] = (prod, b_sb)
+            for jl in range(4):
+                cols = slice(half * BANK + jl * P, half * BANK + (jl + 1) * P)
+                pair = 2 * b + half + jl
+                a_ps, b_ps = bank("a_ps", 2 * pair), bank("b_ps", 2 * pair + 1)
+                for a in range(PASSES):
+                    nc.tensor.matmul_mx(
+                        out=b_ps[:],
+                        lhsT=v_w[a][:, cols].bitcast(FP8X4),
+                        lhsT_scale=(v_sc, v_sc1)[a][:, cols],
+                        rhs=w4_w[:, a, 2 * b * PASS : 2 * (b + 1) * PASS].bitcast(FP4X4),
+                        rhs_scale=w4_sc[:, a, b * PASS : (b + 1) * PASS],
+                        start=(a == 0),
+                        stop=(a == PASSES - 1),
+                    )
+                    nc.tensor.matmul_mx(
+                        out=a_ps[:],
+                        lhsT=v_w[a][:, cols].bitcast(FP8X4),
+                        lhsT_scale=(v_sc, v_sc1)[a][:, cols],
+                        rhs=w1_codes[(b, a)][:].bitcast(FP8X4),
+                        rhs_scale=w1_sc[(b, a)][:],
+                        start=(a == 0),
+                        stop=(a == PASSES - 1),
+                    )
+                nc.scalar.copy(
+                    b_sb[:, jl, :].rearrange("p (t q) -> p t q", t=PACK), b_ps[:].rearrange("p (q t) -> p t q", t=PACK)
+                )
+                nc.vector.scalar_tensor_tensor(
+                    out=prod[:, jl, :].rearrange("p (t q) -> p t q", t=PACK),
+                    in0=b_sb[:, jl, :].rearrange("p (t q) -> p t q", t=PACK),
+                    scalar=1.0,
+                    in1=a_ps[:].rearrange("p (q t) -> p t q", t=PACK),
+                    op0=ALU.add,
+                    op1=ALU.mult,
+                )
+
+        def turn(b, t, half, number):
+            if half == 0:
+                h[(b, t)] = keep.tile([P, S], F32, name="h%d%d" % (b, t), tag="h", bufs=3)
+            h_ps = bank("h_ps", number)
+            for jl in range(4):
+                for which in range(2):
+                    nc.tensor.matmul(
+                        h_ps[:, jl * P : (jl + 1) * P],
+                        lhsT=terms[(b, half)][which][:, jl, t * P : (t + 1) * P],
+                        rhs=ident[:],
+                        is_transpose=True,
+                        start=(which == 0),
+                        stop=(which == 1),
+                    )
+            nc.scalar.activation(h[(b, t)][:, half * BANK : (half + 1) * BANK], h_ps[:], COPY, scale=gain[:, b, t : t + 1])
+
+        def scatter(b, t, first, count):
+            cols = slice(first, first + count)
+            nc.vector.tensor_tensor(
+                pages[t % 2][:].indirect(entries(put, first, count)), h[(b, t)][:, cols], wgs_sb[:, cols], ALU.mult
+            )
+
+        x = {}
+
+        def gather(b, t, first, count):
+            cols = slice(first, first + count)
+            if first == 0:
+                x[(b, t)] = keep.tile([P, M], F32, name="x%d%d" % (b, t), tag="x", bufs=2)
+            nc.vector.tensor_tensor(
+                x[(b, t)][:, cols], pages[t % 2][:].indirect(entries(read, first, count)), wgt_sb[:, cols], ALU.mult
+            )
+
+        z_rows, z_grouped, z_codes, z_sc = {}, {}, {}, {}
+
+        def limit(b, t, first, count):
+            cols = slice(first, first + count)
+            if t == 0:
+                z_rows[b] = keep.tile([P, PACK, M], BF16, name="z_rows%d" % b, tag="slot1%d" % b, align_bytes=64)
+                z_grouped[b] = keep.tile([P, M, PACK], BF16, name="z_grouped%d" % b, align_bytes=64)
+                z_codes[b] = keep.tile([P, M], U32, name="z_codes%d" % b, align_bytes=64)
+                z_sc[b] = keep.tile([P, M], U8, name="z_sc%d" % b, align_bytes=64)
+            nc.vector.tensor_tensor(z_rows[b][:, t, cols], x[(b, t)][:, cols], lim_sb[b][:, t, cols], ALU.min)
+
+        def interleave(b, rows, first, count):
+            cols = slice(first, first + count)
+            nc.scalar.copy(z_grouped[b][:, cols, rows], z_rows[b][:, rows, cols].rearrange("p t m -> p m t"))
+
+        def quantise_z(b, first, count):
+            cols = slice(first, first + count)
+            nc.vector.quantize_mx(
+                out=z_codes[b][:, cols].bitcast(FP8X4),
+                scales=z_sc[b][:, cols],
+                in_=z_grouped[b][:, cols, :].rearrange("p m t -> p (m t)"),
+            )
+
+        def second_pass(acc, b, nb, first):
+            cols = slice(first, first + TAIL)
+            nc.tensor.matmul_mx(
+                out=acc,
+                lhsT=w2_w[:, b, nb * P : (nb + 1) * P].bitcast(FP8X4),
+                lhsT_scale=w2_sc[4 * b : P, nb * P : (nb + 1) * P],
+                rhs=z_codes[b][:, cols].bitcast(FP8X4),
+                rhs_scale=z_sc[b][:, cols],
+                start=(b == 0),
+                stop=(b == PASSES - 1),
+            )
+
+        slices = [(b, t) for b in range(PASSES) for t in range(PACK)]
+        for half in range(2):
+            first_stage(0, half)
+            for t in range(2):
+                turn(0, t, half, 2 * half + t)
+            if half == 1:
+                for a in range(PASSES):
+                    quantise_w1(1, a)
+            for t in range(2):
+                scatter(0, t, half * BANK, BANK)
+        gather(0, 0, 0, M)
+        gather(0, 1, 0, M)
+        limit(0, 0, 0, M)
+        last = PASSES - 1
+        for i in range(2, len(slices)):
+            if i < PACK:
+                first_stage(1, i - 2)
+            for half in range(2):
+                turn(*slices[i], half, 2 * i + half)
+            scatter(*slices[i], 0, S)
+            limit(*slices[i - 1], 0, M)
+            if slices[i - 1] == (0, PACK - 1):
+                interleave(0, slice(0, PACK), 0, M)
+            if slices[i - 1] == (1, 0):
+                quantise_z(0, 0, M)
+            if slices[i - 1] == (last, 1):
+                interleave(last, slice(0, 2), 0, M)
+            if i + 1 < len(slices):
+                gather(*slices[i], 0, M)
+        chunks = M // TAIL
+        accs = {}
+
+        def open_chunk(c):
+            accs[c] = [bank("out_ps", 4 * c + nb) for nb in range(N // P)]
+            for nb in range(N // P):
+                second_pass(accs[c][nb][:, 0:TAIL], 0, nb, c * TAIL)
+
+        def finish(c):
+            quantise_z(last, c * TAIL, TAIL)
+            staged = keep.tile([P, N // P, TAIL], F32, name="staged%d" % c, tag="prod", bufs=4)
+            for nb in range(N // P):
+                second_pass(accs[c][nb][:, 0:TAIL], last, nb, c * TAIL)
+            for nb in range(N // P):
+                if c == chunks - 1 and nb % 2:
+                    nc.vector.tensor_copy(staged[:, nb, :], accs[c][nb][:, 0:TAIL])
+                else:
+                    nc.scalar.copy(staged[:, nb, :], accs[c][nb][:, 0:TAIL])
+            nc.sync.dma_start(out[:, c * TAIL : (c + 1) * TAIL].rearrange("(n p) m -> p n m", p=P), staged[:])
+            if c + 2 < chunks:
+                open_chunk(c + 2)
+
+        open_chunk(0)
+        open_chunk(1)
+        gather(last, PACK - 1, 0, TAIL)
+        for c in range(chunks):
+            if c + 1 < chunks:
+                gather(last, PACK - 1, (c + 1) * TAIL, TAIL)
+            limit(last, PACK - 1, c * TAIL, TAIL)
+            interleave(last, slice(2, PACK), c * TAIL, TAIL)
+            if c >= 1:
+                finish(c - 1)
+        finish(chunks - 1)

@@ -23,7 +23,7 @@ PASS = P * PACK
 PASSES = K // PASS
 BANK = 512
 PER_COL = 16
-TAIL = 256
+TAIL = [256, 256, 256, 128, 128]
 
 
 def tile_list_oyster_flush_scores_kernel(
@@ -45,17 +45,18 @@ def tile_list_oyster_flush_scores_kernel(
         put = lists.tile([P, S // PER_COL], U16, name="put")
         read = lists.tile([P, M // PER_COL], U16, name="read")
 
-        tab_sc = keep.tile([P, T], U8, name="tab_sc", align_bytes=64)
+        tab_sc = keep.tile([P, PASSES, T], U8, name="tab_sc", align_bytes=64)
         w4_sc = keep.tile([P, PASSES, H], U8, name="w4_sc", align_bytes=64)
         w2_sc = keep.tile([P, N], U8, name="w2_sc", align_bytes=64)
-        v_sc = keep.tile([P, S], U8, name="v_sc", align_bytes=64)
-        v_sc1 = keep.tile([P, S], U8, name="v_sc1", align_bytes=64)
+        v_sc = [keep.tile([P, S], U8, name="v_sc%d" % a, align_bytes=64) for a in range(PASSES)]
+        pages = [keep.tile([P, T2], F32, name="page%d" % i) for i in range(2)]
         ident = keep.tile([P, P], F32, name="ident")
 
-        nc.vector.memset(tab_sc[:].bitcast(I32), 0)
+        nc.vector.memset(tab_sc[:].rearrange("p a n -> p (a n)").bitcast(I32), 0)
         nc.vector.memset(w4_sc[:].rearrange("p a n -> p (a n)").bitcast(I32), 0)
-        nc.vector.memset(v_sc1[:].bitcast(I32), 0)
         nc.vector.memset(w2_sc[:].bitcast(I32), 0)
+        for page in pages:
+            nc.vector.memset(page[:], 0.0)
         make_identity(nc, ident[:])
 
         def load_words(a):
@@ -64,24 +65,34 @@ def tile_list_oyster_flush_scores_kernel(
             return words
 
         def load_w1(b, a):
-            raw = keep.tile([P, PACK, BANK], F32, name="w1_raw%d%d" % (b, a), tag="slot%d%d" % (b, a), align_bytes=64)
+            raw = keep.tile([P, PACK, BANK], F32, name="w1_raw%d%d" % (b, a), tag="mid", bufs=4, align_bytes=64)
             nc.sync.dma_start(
                 raw[:], w1[a * PASS : (a + 1) * PASS, b * PASS : (b + 1) * PASS].rearrange("(p i) c -> p i c", i=PACK)
             )
             return raw
 
+        def load_w4(b):
+            words = keep.tile([P, PASSES, 2 * PASS], U8, name="w4_w%d" % b, align_bytes=64)
+            nc.sync.dma_start(
+                words[:].bitcast(I32),
+                w4_words[:, :, 2 * b * PASS : 2 * (b + 1) * PASS].rearrange("a p c -> p a c").bitcast(I32),
+            )
+            return words
+
         nc.sync.dma_start(pick[:], offs)
         tab_w = [load_words(0)]
         for q in range(4):
-            nc.gpsimd.dma_start(tab_sc[32 * q : 32 * q + 8, :].bitcast(I32), tab_scales[:, 4 * q : 4 * q + 4, :].bitcast(I32))
+            nc.sync.dma_start(
+                tab_sc[32 * q : 32 * q + 4, :, :].bitcast(I32),
+                tab_scales[:, 4 * q : 4 * q + 4, :].rearrange("a r n -> r a n").bitcast(I32),
+            )
         w1_raw = {(0, a): load_w1(0, a) for a in range(PASSES)}
         for q in range(4):
-            nc.gpsimd.dma_start(
+            nc.sync.dma_start(
                 w4_sc[32 * q : 32 * q + 4, :, :].bitcast(I32),
                 w4_scales[:, 4 * q : 4 * q + 4, :].rearrange("a r n -> r a n").bitcast(I32),
             )
-        w4_w = keep.tile([P, PASSES, 2 * H], U8, name="w4_w", align_bytes=64)
-        nc.sync.dma_start(w4_w[:].bitcast(I32), w4_words.rearrange("a p c -> p a c").bitcast(I32))
+        w4_w = [load_w4(0)]
         tab_w.append(load_words(1))
         gain = keep.tile([P, PASSES, PACK], F32, name="gain")
         nc.sync.dma_start(gain[:], vigour.rearrange("(b p t) -> p b t", p=P, t=PACK))
@@ -90,14 +101,15 @@ def tile_list_oyster_flush_scores_kernel(
         nc.sync.dma_start(wgs_sb[:], wgs)
         for a in range(PASSES):
             w1_raw[(1, a)] = load_w1(1, a)
+        w4_w.append(load_w4(1))
         nc.sync.dma_start(read[:], offs3)
         wgt_sb = keep.tile([P, M], F32, name="wgt_sb")
         nc.sync.dma_start(wgt_sb[:], wgt)
 
         v_w = [keep.tile([P, S], U32, name="v_w%d" % a, align_bytes=64) for a in range(PASSES)]
-        nc.vector.tensor_copy(v_sc[:], tab_sc[:].indirect(pick[:]))
-        nc.gpsimd.dma_start(v_sc1[0:124, :].bitcast(I32), v_sc[4:128, :].bitcast(I32))
         nc.vector.tensor_copy(v_w[0][:], tab_w[0][:].bitcast(U32).indirect(pick[:]))
+        for a in range(PASSES):
+            nc.vector.tensor_copy(v_sc[a][:], tab_sc[:, a, :].indirect(pick[:]))
 
         w1_codes, w1_sc = {}, {}
 
@@ -110,11 +122,8 @@ def tile_list_oyster_flush_scores_kernel(
                 out=w1_codes[(b, a)][:].bitcast(FP8X4), scales=w1_sc[(b, a)][:], in_=grouped[:].rearrange("p c i -> p (c i)")
             )
 
-        pages = []
         for a in range(PASSES):
             quantise_w1(0, a)
-            pages.append(keep.tile([P, T2], F32, name="page%d" % a, tag="slot0%d" % a, align_bytes=64))
-            nc.vector.memset(pages[a][:], 0.0)
         for half in range(2):
             nc.vector.tensor_copy(
                 v_w[1][:, half * BANK : (half + 1) * BANK], tab_w[1][:].bitcast(U32).indirect(entries(pick, half * BANK, BANK))
@@ -144,8 +153,8 @@ def tile_list_oyster_flush_scores_kernel(
                     nc.tensor.matmul_mx(
                         out=b_ps[:],
                         lhsT=v_w[a][:, cols].bitcast(FP8X4),
-                        lhsT_scale=(v_sc, v_sc1)[a][:, cols],
-                        rhs=w4_w[:, a, 2 * b * PASS : 2 * (b + 1) * PASS].bitcast(FP4X4),
+                        lhsT_scale=v_sc[a][:, cols],
+                        rhs=w4_w[b][:, a, :].bitcast(FP4X4),
                         rhs_scale=w4_sc[:, a, b * PASS : (b + 1) * PASS],
                         start=(a == 0),
                         stop=(a == PASSES - 1),
@@ -153,7 +162,7 @@ def tile_list_oyster_flush_scores_kernel(
                     nc.tensor.matmul_mx(
                         out=a_ps[:],
                         lhsT=v_w[a][:, cols].bitcast(FP8X4),
-                        lhsT_scale=(v_sc, v_sc1)[a][:, cols],
+                        lhsT_scale=v_sc[a][:, cols],
                         rhs=w1_codes[(b, a)][:].bitcast(FP8X4),
                         rhs_scale=w1_sc[(b, a)][:],
                         start=(a == 0),
@@ -197,7 +206,7 @@ def tile_list_oyster_flush_scores_kernel(
 
         def gather(b, t, first, count):
             cols = slice(first, first + count)
-            if first == 0:
+            if (b, t) not in x:
                 x[(b, t)] = keep.tile([P, M], F32, name="x%d%d" % (b, t), tag="x", bufs=2)
             nc.vector.tensor_tensor(
                 x[(b, t)][:, cols], pages[t % 2][:].indirect(entries(read, first, count)), wgt_sb[:, cols], ALU.mult
@@ -208,8 +217,8 @@ def tile_list_oyster_flush_scores_kernel(
         def limit(b, t, first, count):
             cols = slice(first, first + count)
             if t == 0:
-                z_rows[b] = keep.tile([P, PACK, M], BF16, name="z_rows%d" % b, tag="slot1%d" % b, align_bytes=64)
-                z_grouped[b] = keep.tile([P, M, PACK], BF16, name="z_grouped%d" % b, align_bytes=64)
+                z_rows[b] = keep.tile([P, PACK, M], BF16, name="z_rows%d" % b, tag="mid", bufs=4, align_bytes=64)
+                z_grouped[b] = keep.tile([P, M, PACK], BF16, name="z_grouped%d" % b, tag="mid", bufs=4, align_bytes=64)
                 z_codes[b] = keep.tile([P, M], U32, name="z_codes%d" % b, align_bytes=64)
                 z_sc[b] = keep.tile([P, M], U8, name="z_sc%d" % b, align_bytes=64)
             nc.vector.tensor_tensor(z_rows[b][:, t, cols], x[(b, t)][:, cols], lim_sb[b][:, t, cols], ALU.min)
@@ -226,8 +235,8 @@ def tile_list_oyster_flush_scores_kernel(
                 in_=z_grouped[b][:, cols, :].rearrange("p m t -> p (m t)"),
             )
 
-        def second_pass(acc, b, nb, first):
-            cols = slice(first, first + TAIL)
+        def second_pass(acc, b, nb, first, count):
+            cols = slice(first, first + count)
             nc.tensor.matmul_mx(
                 out=acc,
                 lhsT=w2_w[:, b, nb * P : (nb + 1) * P].bitcast(FP8X4),
@@ -258,45 +267,57 @@ def tile_list_oyster_flush_scores_kernel(
             for half in range(2):
                 turn(*slices[i], half, 2 * i + half)
             scatter(*slices[i], 0, S)
-            limit(*slices[i - 1], 0, M)
+            if i + 1 < len(slices):
+                limit(*slices[i - 1], 0, M)
             if slices[i - 1] == (0, PACK - 1):
                 interleave(0, slice(0, PACK), 0, M)
             if slices[i - 1] == (1, 0):
                 quantise_z(0, 0, M)
             if slices[i - 1] == (last, 1):
                 interleave(last, slice(0, 2), 0, M)
+                x_pair = keep.tile([P, 2, M], F32, name="x_pair", tag="b_sb", bufs=4)
+                for t in range(2, PACK):
+                    x[(last, t)] = x_pair[:, t - 2, :]
             if i + 1 < len(slices):
                 gather(*slices[i], 0, M)
-        chunks = M // TAIL
+        starts = [sum(TAIL[:c]) for c in range(len(TAIL))]
         accs = {}
 
         def open_chunk(c):
             accs[c] = [bank("out_ps", 4 * c + nb) for nb in range(N // P)]
             for nb in range(N // P):
-                second_pass(accs[c][nb][:, 0:TAIL], 0, nb, c * TAIL)
+                second_pass(accs[c][nb][:, 0 : TAIL[c]], 0, nb, starts[c], TAIL[c])
+
+        def limit_pair(first, count):
+            cols = slice(first, first + count)
+            nc.vector.tensor_tensor(
+                z_grouped[last][:, cols, 2:PACK],
+                x_pair[:, :, cols].rearrange("p t m -> p m t"),
+                lim_sb[last][:, 2:PACK, cols].rearrange("p t m -> p m t"),
+                ALU.min,
+            )
 
         def finish(c):
-            quantise_z(last, c * TAIL, TAIL)
-            staged = keep.tile([P, N // P, TAIL], F32, name="staged%d" % c, tag="prod", bufs=4)
+            quantise_z(last, starts[c], TAIL[c])
+            staged = keep.tile([P, N // P, TAIL[c]], F32, name="staged%d" % c, tag="prod", bufs=4)
             for nb in range(N // P):
-                second_pass(accs[c][nb][:, 0:TAIL], last, nb, c * TAIL)
+                second_pass(accs[c][nb][:, 0 : TAIL[c]], last, nb, starts[c], TAIL[c])
             for nb in range(N // P):
-                if c == chunks - 1 and nb % 2:
-                    nc.vector.tensor_copy(staged[:, nb, :], accs[c][nb][:, 0:TAIL])
+                if c == len(TAIL) - 1 and nb % 2:
+                    nc.vector.tensor_copy(staged[:, nb, :], accs[c][nb][:, 0 : TAIL[c]])
                 else:
-                    nc.scalar.copy(staged[:, nb, :], accs[c][nb][:, 0:TAIL])
-            nc.sync.dma_start(out[:, c * TAIL : (c + 1) * TAIL].rearrange("(n p) m -> p n m", p=P), staged[:])
-            if c + 2 < chunks:
+                    nc.scalar.copy(staged[:, nb, :], accs[c][nb][:, 0 : TAIL[c]])
+            nc.sync.dma_start(out[:, starts[c] : starts[c] + TAIL[c]].rearrange("(n p) m -> p n m", p=P), staged[:])
+            if c + 2 < len(TAIL):
                 open_chunk(c + 2)
 
         open_chunk(0)
         open_chunk(1)
-        gather(last, PACK - 1, 0, TAIL)
-        for c in range(chunks):
-            if c + 1 < chunks:
-                gather(last, PACK - 1, (c + 1) * TAIL, TAIL)
-            limit(last, PACK - 1, c * TAIL, TAIL)
-            interleave(last, slice(2, PACK), c * TAIL, TAIL)
+        gather(last, PACK - 1, starts[0], TAIL[0])
+        for c in range(len(TAIL)):
+            if c + 1 < len(TAIL):
+                gather(last, PACK - 1, starts[c + 1], TAIL[c + 1])
+            limit_pair(starts[c], TAIL[c])
             if c >= 1:
                 finish(c - 1)
-        finish(chunks - 1)
+        finish(len(TAIL) - 1)

@@ -45,15 +45,16 @@ def tile_list_oyster_flush_scores_kernel(
         put = lists.tile([P, S // PER_COL], U16, name="put")
         read = lists.tile([P, M // PER_COL], U16, name="read")
 
-        tab_sc = keep.tile([P, PASSES, T], U8, name="tab_sc", align_bytes=64)
+        tab_sc = keep.tile([P, T], U8, name="tab_sc", align_bytes=64)
         w4_sc = keep.tile([P, PASSES, H], U8, name="w4_sc", align_bytes=64)
         w2_sc = keep.tile([P, N], U8, name="w2_sc", align_bytes=64)
         v_sc = [keep.tile([P, S], U8, name="v_sc%d" % a, align_bytes=64) for a in range(PASSES)]
         pages = [keep.tile([P, T2], F32, name="page%d" % i) for i in range(2)]
         ident = keep.tile([P, P], F32, name="ident")
 
-        nc.vector.memset(tab_sc[:].rearrange("p a n -> p (a n)").bitcast(I32), 0)
+        nc.vector.memset(tab_sc[:].bitcast(I32), 0)
         nc.vector.memset(w4_sc[:].rearrange("p a n -> p (a n)").bitcast(I32), 0)
+        nc.vector.memset(v_sc[1][:].bitcast(I32), 0)
         nc.vector.memset(w2_sc[:].bitcast(I32), 0)
         for page in pages:
             nc.vector.memset(page[:], 0.0)
@@ -82,10 +83,7 @@ def tile_list_oyster_flush_scores_kernel(
         nc.sync.dma_start(pick[:], offs)
         tab_w = [load_words(0)]
         for q in range(4):
-            nc.sync.dma_start(
-                tab_sc[32 * q : 32 * q + 4, :, :].bitcast(I32),
-                tab_scales[:, 4 * q : 4 * q + 4, :].rearrange("a r n -> r a n").bitcast(I32),
-            )
+            nc.sync.dma_start(tab_sc[32 * q : 32 * q + 8, :].bitcast(I32), tab_scales[:, 4 * q : 4 * q + 4, :].bitcast(I32))
         w1_raw = {(0, a): load_w1(0, a) for a in range(PASSES)}
         for q in range(4):
             nc.sync.dma_start(
@@ -94,6 +92,8 @@ def tile_list_oyster_flush_scores_kernel(
             )
         w4_w = [load_w4(0)]
         tab_w.append(load_words(1))
+        nc.vector.tensor_copy(v_sc[0][:], tab_sc[:].indirect(pick[:]))
+        nc.sync.dma_start(v_sc[1][0 : P - 4, :].bitcast(I32), v_sc[0][4:P, :].bitcast(I32))
         gain = keep.tile([P, PASSES, PACK], F32, name="gain")
         nc.sync.dma_start(gain[:], vigour.rearrange("(b p t) -> p b t", p=P, t=PACK))
         nc.sync.dma_start(put[:], offs2)
@@ -108,14 +108,15 @@ def tile_list_oyster_flush_scores_kernel(
 
         v_w = [keep.tile([P, S], U32, name="v_w%d" % a, align_bytes=64) for a in range(PASSES)]
         nc.vector.tensor_copy(v_w[0][:], tab_w[0][:].bitcast(U32).indirect(pick[:]))
-        for a in range(PASSES):
-            nc.vector.tensor_copy(v_sc[a][:], tab_sc[:, a, :].indirect(pick[:]))
 
         w1_codes, w1_sc = {}, {}
 
         def quantise_w1(b, a):
             grouped = keep.tile([P, BANK, PACK], BF16, name="w1_bf%d%d" % (b, a), tag="w1_bf", bufs=2, align_bytes=64)
-            nc.scalar.copy(grouped[:], w1_raw[(b, a)][:].rearrange("p i c -> p c i"))
+            nc.scalar.copy(
+                grouped[:].rearrange("p (t q) i -> p q i t", t=PACK),
+                w1_raw[(b, a)][:].rearrange("p i (q t) -> p q i t", t=PACK),
+            )
             w1_codes[(b, a)] = keep.tile([P, BANK], U32, name="w1_codes%d%d" % (b, a), align_bytes=64)
             w1_sc[(b, a)] = keep.tile([P, BANK], U8, name="w1_sc%d%d" % (b, a), align_bytes=64)
             nc.vector.quantize_mx(
@@ -169,13 +170,13 @@ def tile_list_oyster_flush_scores_kernel(
                         stop=(a == PASSES - 1),
                     )
                 nc.scalar.copy(
-                    b_sb[:, jl, :].rearrange("p (t q) -> p t q", t=PACK), b_ps[:].rearrange("p (q t) -> p t q", t=PACK)
+                    b_sb[:, jl, :].rearrange("p (t q) -> p q t", t=PACK), b_ps[:].rearrange("p (q t) -> p q t", t=PACK)
                 )
                 nc.vector.scalar_tensor_tensor(
-                    out=prod[:, jl, :].rearrange("p (t q) -> p t q", t=PACK),
-                    in0=b_sb[:, jl, :].rearrange("p (t q) -> p t q", t=PACK),
+                    out=prod[:, jl, :],
+                    in0=b_sb[:, jl, :],
                     scalar=1.0,
-                    in1=a_ps[:].rearrange("p (q t) -> p t q", t=PACK),
+                    in1=a_ps[:],
                     op0=ALU.add,
                     op1=ALU.mult,
                 )

@@ -181,11 +181,12 @@ def tile_list_oyster_flush_scores_kernel(
                     op1=ALU.mult,
                 )
 
-        def turn(b, t, half, number):
-            if half == 0:
+        def turn(b, t, first, count, number):
+            half, blocks = first // BANK, range(first % BANK // P, (first % BANK + count) // P)
+            if first == 0:
                 h[(b, t)] = keep.tile([P, S], F32, name="h%d%d" % (b, t), tag="h", bufs=3)
             h_ps = bank("h_ps", number)
-            for jl in range(4):
+            for jl in blocks:
                 for which in range(2):
                     nc.tensor.matmul(
                         h_ps[:, jl * P : (jl + 1) * P],
@@ -195,7 +196,12 @@ def tile_list_oyster_flush_scores_kernel(
                         start=(which == 0),
                         stop=(which == 1),
                     )
-            nc.scalar.activation(h[(b, t)][:, half * BANK : (half + 1) * BANK], h_ps[:], COPY, scale=gain[:, b, t : t + 1])
+            nc.scalar.activation(
+                h[(b, t)][:, first : first + count],
+                h_ps[:, first % BANK : first % BANK + count],
+                COPY,
+                scale=gain[:, b, t : t + 1],
+            )
 
         def scatter(b, t, first, count):
             cols = slice(first, first + count)
@@ -215,14 +221,22 @@ def tile_list_oyster_flush_scores_kernel(
 
         z_rows, z_grouped, z_codes, z_sc = {}, {}, {}, {}
 
-        def limit(b, t, first, count):
-            cols = slice(first, first + count)
+        lim_bf = {}
+
+        def round_rows(b, t):
             if t == 0:
                 z_rows[b] = keep.tile([P, PACK, M], BF16, name="z_rows%d" % b, tag="mid", bufs=4, align_bytes=64)
                 z_grouped[b] = keep.tile([P, M, PACK], BF16, name="z_grouped%d" % b, tag="mid", bufs=4, align_bytes=64)
                 z_codes[b] = keep.tile([P, M], U32, name="z_codes%d" % b, align_bytes=64)
                 z_sc[b] = keep.tile([P, M], U8, name="z_sc%d" % b, align_bytes=64)
-            nc.vector.tensor_tensor(z_rows[b][:, t, cols], x[(b, t)][:, cols], lim_sb[b][:, t, cols], ALU.min)
+            if t % 2 == 0:
+                lim_bf[(b, t // 2)] = keep.tile([P, 2, M], BF16, name="lim_bf%d%d" % (b, t), tag="w1_bf", bufs=2, align_bytes=64)
+                nc.scalar.copy(lim_bf[(b, t // 2)][:], lim_sb[b][:, t : t + 2, :])
+            nc.scalar.copy(z_rows[b][:, t, :], x[(b, t)][:])
+
+        def limit(b, pair):
+            rows = z_rows[b][:, 2 * pair : 2 * pair + 2, :]
+            nc.vector.tensor_tensor(rows, rows, lim_bf[(b, pair)][:], ALU.min)
 
         def interleave(b, rows, first, count):
             cols = slice(first, first + count)
@@ -251,36 +265,40 @@ def tile_list_oyster_flush_scores_kernel(
         slices = [(b, t) for b in range(PASSES) for t in range(PACK)]
         for half in range(2):
             first_stage(0, half)
-            for t in range(2):
-                turn(0, t, half, 2 * half + t)
+            pieces = [(0, half * BANK, BANK // 2), (1, half * BANK, BANK), (0, half * BANK + BANK // 2, BANK // 2)]
+            for t, first, count in pieces:
+                turn(0, t, first, count, 2 * half + t)
             if half == 1:
                 for a in range(PASSES):
                     quantise_w1(1, a)
-            for t in range(2):
-                scatter(0, t, half * BANK, BANK)
-        gather(0, 0, 0, M)
-        gather(0, 1, 0, M)
-        limit(0, 0, 0, M)
+            for t, first, count in pieces:
+                scatter(0, t, first, count)
         last = PASSES - 1
+        for t in range(2):
+            gather(0, t, 0, M)
+            round_rows(0, t)
         for i in range(2, len(slices)):
+            b, t = slices[i]
             if i < PACK:
                 first_stage(1, i - 2)
             for half in range(2):
-                turn(*slices[i], half, 2 * i + half)
-            scatter(*slices[i], 0, S)
-            if i + 1 < len(slices):
-                limit(*slices[i - 1], 0, M)
-            if slices[i - 1] == (0, PACK - 1):
+                turn(b, t, half * BANK, BANK, 2 * i + half)
+            scatter(b, t, 0, S)
+            if i % 2 == 0:
+                limit((i - 2) // PACK, (i - 2) % PACK // 2)
+            if (b, t) == (1, 0):
                 interleave(0, slice(0, PACK), 0, M)
-            if slices[i - 1] == (1, 0):
+            if (b, t) == (1, 1):
                 quantise_z(0, 0, M)
-            if slices[i - 1] == (last, 1):
+            if (b, t) == (last, 2):
                 interleave(last, slice(0, 2), 0, M)
                 x_pair = keep.tile([P, 2, M], F32, name="x_pair", tag="b_sb", bufs=4)
-                for t in range(2, PACK):
-                    x[(last, t)] = x_pair[:, t - 2, :]
+                for u in range(2, PACK):
+                    x[(last, u)] = x_pair[:, u - 2, :]
             if i + 1 < len(slices):
-                gather(*slices[i], 0, M)
+                gather(b, t, 0, M)
+            if i + 2 < len(slices):
+                round_rows(b, t)
         starts = [sum(TAIL[:c]) for c in range(len(TAIL))]
         accs = {}
 

from contextlib import ExitStack

import concourse.mybir as mybir
from concourse.masks import make_identity

K, H, N, T, S, M, T2 = 1024, 1024, 512, 4096, 1024, 1024, 2048
FLOPS = 2 * (2 * K * H * S + H * N * M)

F32 = mybir.dt.float32
BF16 = mybir.dt.bfloat16
I32 = mybir.dt.int32
U32 = mybir.dt.uint32
U16 = mybir.dt.uint16
U8 = mybir.dt.uint8
FP8X4 = mybir.dt.float8_e4m3fn_x4
FP4X4 = mybir.dt.float4_e2m1fn_x4
ALU = mybir.AluOpType
COPY = mybir.ActivationFunctionType.Copy

P = 128
PACK = 4
PASS = P * PACK
PASSES = K // PASS
BANK = 512
PER_COL = 16
TAIL = [256, 256, 256, 128, 128]


def tile_list_oyster_flush_scores_kernel(
    tc, tab_words, tab_scales, offs, offs2, offs3, w1, w4_words, w4_scales, vigour, wgs, wgt, lim, w2_words, w2_scales, out
):
    nc = tc.nc
    with ExitStack() as ctx:
        lists = ctx.enter_context(tc.tile_pool(name="lists", bufs=1))
        keep = ctx.enter_context(tc.tile_pool(name="keep", bufs=1))
        psum = ctx.enter_context(tc.psum_pool(name="psum", bufs=1))

        def bank(name, number):
            return psum.tile([P, BANK], F32, name=name, tag="bank%d" % (number % 8))

        def entries(lst, first, count):
            return lst[:, first // PER_COL : (first + count) // PER_COL]

        pick = lists.tile([P, S // PER_COL], U16, name="pick")
        put = lists.tile([P, S // PER_COL], U16, name="put")
        read = lists.tile([P, M // PER_COL], U16, name="read")

        tab_sc = keep.tile([P, T], U8, name="tab_sc", align_bytes=64)
        w4_sc = keep.tile([P, PASSES, H], U8, name="w4_sc", align_bytes=64)
        w2_sc = keep.tile([P, N], U8, name="w2_sc", align_bytes=64)
        v_sc = [keep.tile([P, S], U8, name="v_sc%d" % a, align_bytes=64) for a in range(PASSES)]
        pages = [keep.tile([P, T2], F32, name="page%d" % i) for i in range(2)]
        ident = keep.tile([P, P], F32, name="ident")

        nc.vector.memset(tab_sc[:].bitcast(I32), 0)
        nc.vector.memset(w4_sc[:].rearrange("p a n -> p (a n)").bitcast(I32), 0)
        nc.vector.memset(v_sc[1][:].bitcast(I32), 0)
        nc.vector.memset(w2_sc[:].bitcast(I32), 0)
        for page in pages:
            nc.vector.memset(page[:], 0.0)
        make_identity(nc, ident[:])

        def load_words(a):
            words = keep.tile([P, T], I32, name="tab_w%d" % a, tag="big", bufs=2)
            nc.sync.dma_start(words[:], tab_words[a].rearrange("p t i -> p (t i)").bitcast(I32))
            return words

        def load_w1(b, a):
            raw = keep.tile([P, PACK, BANK], F32, name="w1_raw%d%d" % (b, a), tag="mid", bufs=4, align_bytes=64)
            nc.sync.dma_start(
                raw[:], w1[a * PASS : (a + 1) * PASS, b * PASS : (b + 1) * PASS].rearrange("(p i) c -> p i c", i=PACK)
            )
            return raw

        def load_w4(b):
            words = keep.tile([P, PASSES, 2 * PASS], U8, name="w4_w%d" % b, align_bytes=64)
            nc.sync.dma_start(
                words[:].bitcast(I32),
                w4_words[:, :, 2 * b * PASS : 2 * (b + 1) * PASS].rearrange("a p c -> p a c").bitcast(I32),
            )
            return words

        nc.sync.dma_start(pick[:], offs)
        tab_w = [load_words(0)]
        for q in range(4):
            nc.sync.dma_start(tab_sc[32 * q : 32 * q + 8, :].bitcast(I32), tab_scales[:, 4 * q : 4 * q + 4, :].bitcast(I32))
        w1_raw = {(0, a): load_w1(0, a) for a in range(PASSES)}
        for q in range(4):
            nc.sync.dma_start(
                w4_sc[32 * q : 32 * q + 4, :, :].bitcast(I32),
                w4_scales[:, 4 * q : 4 * q + 4, :].rearrange("a r n -> r a n").bitcast(I32),
            )
        w4_w = [load_w4(0)]
        tab_w.append(load_words(1))
        nc.vector.tensor_copy(v_sc[0][:], tab_sc[:].indirect(pick[:]))
        nc.sync.dma_start(v_sc[1][0 : P - 4, :].bitcast(I32), v_sc[0][4:P, :].bitcast(I32))
        gain = keep.tile([P, PASSES, PACK], F32, name="gain")
        nc.sync.dma_start(gain[:], vigour.rearrange("(b p t) -> p b t", p=P, t=PACK))
        nc.sync.dma_start(put[:], offs2)
        wgs_sb = keep.tile([P, S], F32, name="wgs_sb")
        nc.sync.dma_start(wgs_sb[:], wgs)
        for a in range(PASSES):
            w1_raw[(1, a)] = load_w1(1, a)
        w4_w.append(load_w4(1))
        nc.sync.dma_start(read[:], offs3)
        wgt_sb = keep.tile([P, M], F32, name="wgt_sb")
        nc.sync.dma_start(wgt_sb[:], wgt)

        v_w = [keep.tile([P, S], U32, name="v_w%d" % a, align_bytes=64) for a in range(PASSES)]
        nc.vector.tensor_copy(v_w[0][:], tab_w[0][:].bitcast(U32).indirect(pick[:]))

        w1_codes, w1_sc = {}, {}

        def quantise_w1(b, a):
            grouped = keep.tile([P, BANK, PACK], BF16, name="w1_bf%d%d" % (b, a), tag="w1_bf", bufs=2, align_bytes=64)
            nc.scalar.copy(
                grouped[:].rearrange("p (t q) i -> p q i t", t=PACK),
                w1_raw[(b, a)][:].rearrange("p i (q t) -> p q i t", t=PACK),
            )
            w1_codes[(b, a)] = keep.tile([P, BANK], U32, name="w1_codes%d%d" % (b, a), align_bytes=64)
            w1_sc[(b, a)] = keep.tile([P, BANK], U8, name="w1_sc%d%d" % (b, a), align_bytes=64)
            nc.vector.quantize_mx(
                out=w1_codes[(b, a)][:].bitcast(FP8X4), scales=w1_sc[(b, a)][:], in_=grouped[:].rearrange("p c i -> p (c i)")
            )

        for a in range(PASSES):
            quantise_w1(0, a)
        for half in range(2):
            nc.vector.tensor_copy(
                v_w[1][:, half * BANK : (half + 1) * BANK], tab_w[1][:].bitcast(U32).indirect(entries(pick, half * BANK, BANK))
            )

        lim_sb = []
        for b in range(PASSES):
            lim_b = keep.tile([P, PACK, M], F32, name="lim%d" % b, tag="big", bufs=2)
            nc.sync.dma_start(lim_b[:], lim[b * PASS : (b + 1) * PASS, :].rearrange("(p t) m -> p t m", t=PACK))
            lim_sb.append(lim_b)
        w2_w = keep.tile([P, PASSES, N], U32, name="w2_w", align_bytes=64)
        nc.sync.dma_start(w2_w[:].bitcast(I32), w2_words.rearrange("a p c i -> p a (c i)").bitcast(I32))
        for q in range(4):
            nc.sync.dma_start(w2_sc[32 * q : 32 * q + 8, :].bitcast(I32), w2_scales[:, 4 * q : 4 * q + 4, :].bitcast(I32))

        h, terms = {}, {}

        def first_stage(b, half):
            prod = keep.tile([P, 4, BANK], F32, name="prod%d%d" % (b, half), tag="prod", bufs=4)
            b_sb = keep.tile([P, 4, BANK], F32, name="b_sb%d%d" % (b, half), tag="b_sb", bufs=4)
            terms[(b, half)] = (prod, b_sb)
            for jl in range(4):
                cols = slice(half * BANK + jl * P, half * BANK + (jl + 1) * P)
                pair = 2 * b + half + jl
                a_ps, b_ps = bank("a_ps", 2 * pair), bank("b_ps", 2 * pair + 1)
                for a in range(PASSES):
                    nc.tensor.matmul_mx(
                        out=b_ps[:],
                        lhsT=v_w[a][:, cols].bitcast(FP8X4),
                        lhsT_scale=v_sc[a][:, cols],
                        rhs=w4_w[b][:, a, :].bitcast(FP4X4),
                        rhs_scale=w4_sc[:, a, b * PASS : (b + 1) * PASS],
                        start=(a == 0),
                        stop=(a == PASSES - 1),
                    )
                    nc.tensor.matmul_mx(
                        out=a_ps[:],
                        lhsT=v_w[a][:, cols].bitcast(FP8X4),
                        lhsT_scale=v_sc[a][:, cols],
                        rhs=w1_codes[(b, a)][:].bitcast(FP8X4),
                        rhs_scale=w1_sc[(b, a)][:],
                        start=(a == 0),
                        stop=(a == PASSES - 1),
                    )
                nc.scalar.copy(
                    b_sb[:, jl, :].rearrange("p (t q) -> p q t", t=PACK), b_ps[:].rearrange("p (q t) -> p q t", t=PACK)
                )
                nc.vector.scalar_tensor_tensor(
                    out=prod[:, jl, :],
                    in0=b_sb[:, jl, :],
                    scalar=1.0,
                    in1=a_ps[:],
                    op0=ALU.add,
                    op1=ALU.mult,
                )

        def turn(b, t, first, count, number):
            half, blocks = first // BANK, range(first % BANK // P, (first % BANK + count) // P)
            if first == 0:
                h[(b, t)] = keep.tile([P, S], F32, name="h%d%d" % (b, t), tag="h", bufs=3)
            h_ps = bank("h_ps", number)
            for jl in blocks:
                for which in range(2):
                    nc.tensor.matmul(
                        h_ps[:, jl * P : (jl + 1) * P],
                        lhsT=terms[(b, half)][which][:, jl, t * P : (t + 1) * P],
                        rhs=ident[:],
                        is_transpose=True,
                        start=(which == 0),
                        stop=(which == 1),
                    )
            nc.scalar.activation(
                h[(b, t)][:, first : first + count],
                h_ps[:, first % BANK : first % BANK + count],
                COPY,
                scale=gain[:, b, t : t + 1],
            )

        def scatter(b, t, first, count):
            cols = slice(first, first + count)
            nc.vector.tensor_tensor(
                pages[t % 2][:].indirect(entries(put, first, count)), h[(b, t)][:, cols], wgs_sb[:, cols], ALU.mult
            )

        x = {}

        def gather(b, t, first, count):
            cols = slice(first, first + count)
            if (b, t) not in x:
                x[(b, t)] = keep.tile([P, M], F32, name="x%d%d" % (b, t), tag="x", bufs=2)
            nc.vector.tensor_tensor(
                x[(b, t)][:, cols], pages[t % 2][:].indirect(entries(read, first, count)), wgt_sb[:, cols], ALU.mult
            )

        z_rows, z_grouped, z_codes, z_sc = {}, {}, {}, {}

        lim_bf = {}

        def round_rows(b, t):
            if t == 0:
                z_rows[b] = keep.tile([P, PACK, M], BF16, name="z_rows%d" % b, tag="mid", bufs=4, align_bytes=64)
                z_grouped[b] = keep.tile([P, M, PACK], BF16, name="z_grouped%d" % b, tag="mid", bufs=4, align_bytes=64)
                z_codes[b] = keep.tile([P, M], U32, name="z_codes%d" % b, align_bytes=64)
                z_sc[b] = keep.tile([P, M], U8, name="z_sc%d" % b, align_bytes=64)
            if t % 2 == 0:
                lim_bf[(b, t // 2)] = keep.tile([P, 2, M], BF16, name="lim_bf%d%d" % (b, t), tag="w1_bf", bufs=2, align_bytes=64)
                nc.scalar.copy(lim_bf[(b, t // 2)][:], lim_sb[b][:, t : t + 2, :])
            nc.scalar.copy(z_rows[b][:, t, :], x[(b, t)][:])

        def limit(b, pair):
            rows = z_rows[b][:, 2 * pair : 2 * pair + 2, :]
            nc.vector.tensor_tensor(rows, rows, lim_bf[(b, pair)][:], ALU.min)

        def interleave(b, rows, first, count):
            cols = slice(first, first + count)
            nc.scalar.copy(z_grouped[b][:, cols, rows], z_rows[b][:, rows, cols].rearrange("p t m -> p m t"))

        def quantise_z(b, first, count):
            cols = slice(first, first + count)
            nc.vector.quantize_mx(
                out=z_codes[b][:, cols].bitcast(FP8X4),
                scales=z_sc[b][:, cols],
                in_=z_grouped[b][:, cols, :].rearrange("p m t -> p (m t)"),
            )

        def second_pass(acc, b, nb, first, count):
            cols = slice(first, first + count)
            nc.tensor.matmul_mx(
                out=acc,
                lhsT=w2_w[:, b, nb * P : (nb + 1) * P].bitcast(FP8X4),
                lhsT_scale=w2_sc[4 * b : P, nb * P : (nb + 1) * P],
                rhs=z_codes[b][:, cols].bitcast(FP8X4),
                rhs_scale=z_sc[b][:, cols],
                start=(b == 0),
                stop=(b == PASSES - 1),
            )

        slices = [(b, t) for b in range(PASSES) for t in range(PACK)]
        for half in range(2):
            first_stage(0, half)
            pieces = [(0, half * BANK, BANK // 2), (1, half * BANK, BANK), (0, half * BANK + BANK // 2, BANK // 2)]
            for t, first, count in pieces:
                turn(0, t, first, count, 2 * half + t)
            if half == 1:
                for a in range(PASSES):
                    quantise_w1(1, a)
            for t, first, count in pieces:
                scatter(0, t, first, count)
        last = PASSES - 1
        for t in range(2):
            gather(0, t, 0, M)
            round_rows(0, t)
        for i in range(2, len(slices)):
            b, t = slices[i]
            if i < PACK:
                first_stage(1, i - 2)
            for half in range(2):
                turn(b, t, half * BANK, BANK, 2 * i + half)
            scatter(b, t, 0, S)
            if i % 2 == 0:
                limit((i - 2) // PACK, (i - 2) % PACK // 2)
            if (b, t) == (1, 0):
                interleave(0, slice(0, PACK), 0, M)
            if (b, t) == (1, 1):
                quantise_z(0, 0, M)
            if (b, t) == (last, 2):
                interleave(last, slice(0, 2), 0, M)
                x_pair = keep.tile([P, 2, M], F32, name="x_pair", tag="b_sb", bufs=4)
                for u in range(2, PACK):
                    x[(last, u)] = x_pair[:, u - 2, :]
            if i + 1 < len(slices):
                gather(b, t, 0, M)
            if i + 2 < len(slices):
                round_rows(b, t)
        starts = [sum(TAIL[:c]) for c in range(len(TAIL))]
        accs = {}

        def open_chunk(c):
            accs[c] = [bank("out_ps", 4 * c + nb) for nb in range(N // P)]
            for nb in range(N // P):
                second_pass(accs[c][nb][:, 0 : TAIL[c]], 0, nb, starts[c], TAIL[c])

        def limit_pair(first, count):
            cols = slice(first, first + count)
            nc.vector.tensor_tensor(
                z_grouped[last][:, cols, 2:PACK],
                x_pair[:, :, cols].rearrange("p t m -> p m t"),
                lim_sb[last][:, 2:PACK, cols].rearrange("p t m -> p m t"),
                ALU.min,
            )

        def finish(c):
            quantise_z(last, starts[c], TAIL[c])
            staged = keep.tile([P, N // P, TAIL[c]], F32, name="staged%d" % c, tag="prod", bufs=4)
            for nb in range(N // P):
                second_pass(accs[c][nb][:, 0 : TAIL[c]], last, nb, starts[c], TAIL[c])
            for nb in range(N // P):
                if c == len(TAIL) - 1 and nb % 2:
                    nc.vector.tensor_copy(staged[:, nb, :], accs[c][nb][:, 0 : TAIL[c]])
                else:
                    nc.scalar.copy(staged[:, nb, :], accs[c][nb][:, 0 : TAIL[c]])
            nc.sync.dma_start(out[:, starts[c] : starts[c] + TAIL[c]].rearrange("(n p) m -> p n m", p=P), staged[:])
            if c + 2 < len(TAIL):
                open_chunk(c + 2)

        open_chunk(0)
        open_chunk(1)
        gather(last, PACK - 1, starts[0], TAIL[0])
        for c in range(len(TAIL)):
            if c + 1 < len(TAIL):
                gather(last, PACK - 1, starts[c + 1], TAIL[c + 1])
            limit_pair(starts[c], TAIL[c])
            if c >= 1:
                finish(c - 1)
        finish(len(TAIL) - 1)
